import numpy as np
import ml_dtypes


def mxq(x, axis, fmt="e4m3"):
    dtype, down = {"e4m3": (ml_dtypes.float8_e4m3fn, 7), "e5m2": (ml_dtypes.float8_e5m2, 14)}[fmt]
    v = np.moveaxis(np.asarray(x, np.float32).astype(ml_dtypes.bfloat16).astype(np.float64), axis, -1)
    blocks = v.reshape(v.shape[:-1] + (-1, 32))
    amax = np.abs(blocks).max(-1, keepdims=True)
    byte = np.maximum(np.where(amax > 0, np.frexp(amax)[1] - 1 + 127, 0) - down, 1)
    scale = np.exp2(byte - 127.0)
    codes = (blocks / scale).astype(np.float32).astype(dtype).astype(np.float64)
    return np.moveaxis((codes * scale).reshape(v.shape), -1, axis)


WIDE = False


def mx_kscale(k):
    if not WIDE:
        return np.ones(k)
    levels = np.array([10, -10, 5, -5, 0])
    if k % 512:
        return np.exp2(np.random.permutation(np.resize(levels, k // 32))).repeat(32)
    a = np.empty((k // 512, 16))
    for p in range(k // 512):
        a[p, :8] = np.random.permutation(np.resize(levels, 8))
        for g in range(8):
            far = levels[np.abs(levels - a[p, g]) >= 10]
            a[p, g + 8] = far[np.random.randint(len(far))]
    return np.exp2(a.ravel()).repeat(32)


BF16 = ml_dtypes.bfloat16


def bf(x):
    return np.asarray(x, np.float32).astype(BF16)


def f64(x):
    return np.asarray(x).astype(np.float64)


S, F, G, T, C = 1024, 1024, 1024, 512, 512


def smooth_modulus(re, im):
    return np.sqrt(re * re + im * im + 0.25)


def draw0():
    s, t = mx_kscale(S), mx_kscale(F)
    a_scale = 1.0 / np.sqrt(S)
    c_scale = 1.5 / np.sqrt(F)
    return {
        "x": bf(np.random.standard_normal((S, C)) * s[:, None]),
        "ar": bf(np.random.standard_normal((F, S)) * a_scale / s[None, :]),
        "aim": bf(np.random.standard_normal((F, S)) * a_scale / s[None, :]),
        "g1": bf((1.0 + 0.1 * np.random.standard_normal(F)) * t),
        "cr": bf(np.random.standard_normal((G, F)) * c_scale / t[None, :]),
        "cim": bf(np.random.standard_normal((G, F)) * c_scale / t[None, :]),
        "phi": bf(np.random.standard_normal((T, F)) * c_scale / t[None, :]),
    }


def core(x, ar, aim, g1, cr, cim, phi):
    xq = mxq(f64(x), 0, "e4m3")
    r1 = mxq(f64(ar), 1, "e4m3") @ xq
    i1 = mxq(f64(aim), 1, "e4m3") @ xq
    u1 = smooth_modulus(r1, i1)
    n1 = f64(g1)[:, None] * (u1 - np.mean(u1, axis=0, keepdims=True))
    nq = mxq(n1, 0, "e4m3")
    s1 = mxq(f64(phi), 1, "e4m3") @ nq
    r2 = mxq(f64(cr), 1, "e4m3") @ nq
    i2 = mxq(f64(cim), 1, "e4m3") @ nq
    u2 = smooth_modulus(r2, i2)
    return s1, u2


def e4m3fn_bytes(y):
    return np.clip(np.asarray(y, np.float64), -448.0, 448.0).astype(np.float32).astype(ml_dtypes.float8_e4m3fn).view(np.uint8)


def e4m3fn_values(b):
    return np.asarray(b, np.uint8).view(ml_dtypes.float8_e4m3fn).astype(np.float64)


def setup_inputs():
    d = draw0()
    x0 = np.asarray(d['cr']).astype(np.float64)
    s = (np.max(np.abs(x0), axis=(0,), keepdims=True) / 448.0).astype(np.float32)
    out = {}
    for k, v in d.items():
        if k == 'cr':
            out['cr_bytes'] = e4m3fn_bytes(x0 / s.astype(np.float64))
            out['cr_scale'] = s
        else:
            out[k] = v
    return out


def reference(x, ar, aim, g1, cr_bytes, cr_scale, cim, phi):
    return core(x, ar, aim, g1, e4m3fn_values(cr_bytes) * cr_scale.astype(np.float64), cim, phi)

@@ -1,0 +1,294 @@
+from contextlib import ExitStack
+
+import concourse.mybir as mybir
+from concourse.masks import make_identity
+
+S, F, G, T, C = 1024, 1024, 1024, 512, 512
+FLOPS = 2 * C * (2 * F * S + 2 * G * F + T * F)
+
+F32 = mybir.dt.float32
+BF16 = mybir.dt.bfloat16
+U32 = mybir.dt.uint32
+U8 = mybir.dt.uint8
+FP8 = mybir.dt.float8_e4m3fn
+FP8X4 = mybir.dt.float8_e4m3fn_x4
+ACT = mybir.ActivationFunctionType
+ALU = mybir.AluOpType
+P = 128
+PASSES = 2
+QROWS = 256
+WORDS = 512
+
+
+def tile_learnedsecondorderscattering_kernel(tc, x, ar, aim, g1, cr_bytes, cr_scale, cim, phi, out_0, out_1):
+    nc = tc.nc
+    with ExitStack() as ctx:
+        keep = ctx.enter_context(tc.tile_pool(name="keep", bufs=1))
+        stage = ctx.enter_context(tc.tile_pool(name="stage", bufs=1))
+        psum = ctx.enter_context(tc.psum_pool(name="psum", bufs=1))
+        ctx.enter_context(tc.manual_schedule())
+
+        def load_pair(matrix, pair, split):
+            rows = stage.tile([P, 2, S], BF16, name="rows", tag="rows", bufs=10, align_bytes=64)
+            src = matrix[pair * 256 : (pair + 1) * 256, :].rearrange("(b p) k -> p b k", b=2)
+            if split:
+                for b in range(2):
+                    nc.sync.dma_start(out=rows[:, b, :], in_=src[:, b, :])
+            else:
+                nc.sync.dma_start(out=rows[:], in_=src)
+            return rows
+
+        a_rows = {(0, 0): load_pair(ar, 0, True)}
+        x_raw = []
+        for g in range(PASSES):
+            t = keep.tile([P, 4, C], BF16, name="x_raw%d" % g, align_bytes=64)
+            nc.sync.dma_start(out=t[:], in_=x.rearrange("(g p t) n -> g p t n", p=P, t=4)[g])
+            x_raw.append(t)
+        a_rows[1, 0] = load_pair(aim, 0, True)
+        for q in range(1, 4):
+            a_rows[0, q] = load_pair(ar, q, q < 2)
+            a_rows[1, q] = load_pair(aim, q, q < 2)
+        scale = keep.tile([P, F], F32, name="scale", align_bytes=64)
+        nc.sync.dma_start(out=scale[:], in_=cr_scale.rearrange("o k -> (o k)").partition_broadcast(P))
+        gain_flat = keep.tile([P, F], BF16, name="gain_flat", align_bytes=64)
+        nc.sync.dma_start(out=gain_flat[:], in_=g1.partition_broadcast(P))
+        cr_raw = []
+        for h in range(2):
+            t = keep.tile([P, 4, F], U8, name="cr_raw%d" % h, align_bytes=64)
+            nc.sync.dma_start(out=t[:], in_=cr_bytes[h * 512 : (h + 1) * 512, :].rearrange("(b p) k -> p b k", b=4))
+            cr_raw.append(t)
+
+        ident = keep.tile([P, P], F32, name="ident", align_bytes=64)
+        make_identity(nc, ident[:])
+        quarter = keep.tile([P, 1], F32, name="quarter")
+        nc.vector.memset(quarter[:], 0.25)
+        warm = keep.tile([P, 1], F32, name="warm")
+        nc.scalar.activation(out=warm[:], in_=quarter[:], func=ACT.Sqrt)
+
+        def turn_block(words):
+            bank = psum.tile([P, 4, P], F32, name="turned", tag="turned", bufs=4)
+            for g in range(PASSES):
+                for u in range(2):
+                    nc.tensor.transpose(bank[:, 2 * g + u, :], words[:, 256 * g + u : 256 * (g + 1) : 2], ident[:])
+            return bank
+
+        def new_grouped():
+            return stage.tile([P, PASSES, QROWS, 4], BF16, name="grouped", tag="grouped", bufs=6, align_bytes=64)
+
+        def empty_block(engine, bank, grouped, half):
+            dst = grouped[:].rearrange("p g r t -> p (g r t)").bitcast(F32).rearrange("p (g r u) -> p g r u", g=PASSES, u=2)
+            dst = dst[:, :, half * P : (half + 1) * P, :]
+            src = bank[:].rearrange("p (g u) r -> p g r u", u=2)
+            if engine == "S":
+                nc.scalar.copy(out=dst, in_=src)
+            else:
+                nc.vector.tensor_copy(out=dst, in_=src)
+
+        def quantise(flat, tag, bufs):
+            width = flat.shape[1] // 4
+            codes = keep.tile([P, width], U32, name="codes", tag=tag + "_c", bufs=bufs, align_bytes=64)
+            scales = keep.tile([P, width], U8, name="scales", tag=tag + "_s", bufs=bufs, align_bytes=64)
+            nc.vector.quantize_mx(out=codes[:].bitcast(FP8X4), scales=scales[:], in_=flat)
+            return codes, scales
+
+        def quantise_pair(grouped, tag, bufs):
+            return quantise(grouped[:].rearrange("p g r t -> p (g r t)"), tag, bufs)
+
+        def mx(out, lhs, lcols, rhs, rcols, start, stop):
+            nc.tensor.matmul_mx(
+                out=out,
+                lhsT=lhs[0][:, lcols].bitcast(FP8X4),
+                lhsT_scale=lhs[1][:, lcols],
+                rhs=rhs[0][:, rcols].bitcast(FP8X4),
+                rhs_scale=rhs[1][:, rcols],
+                start=start,
+                stop=stop,
+            )
+
+        gain = keep.tile([P, PASSES, 2, 256], BF16, name="gain", align_bytes=64)
+
+        def spread_gain():
+            for g in range(PASSES):
+                nc.vector.tensor_copy(
+                    out=gain[:, g].bitcast(F32),
+                    in_=gain_flat[:, g * 512 : (g + 1) * 512].bitcast(F32).rearrange("p (w u) -> p u w", u=2),
+                )
+
+        x_grouped = [stage.tile([P, C, 4], BF16, name="x_grouped", tag="x_grouped", bufs=2, align_bytes=64) for g in range(PASSES)]
+        nc.vector.tensor_copy(out=x_grouped[0][:], in_=x_raw[0][:].rearrange("p t n -> p n t"))
+        nc.vector.tensor_copy(out=x_grouped[1][:], in_=x_raw[1][:].rearrange("p t n -> p n t"))
+        xq = [quantise(x_grouped[g][:].rearrange("p n t -> p (n t)"), "x", 2) for g in range(PASSES)]
+
+        u1 = [keep.tile([P, PASSES, 2, 256], F32, name="u1_%d" % j, align_bytes=64) for j in range(4)]
+        n1 = [keep.tile([P, PASSES, 2, 256], BF16, name="n1_%d" % j, align_bytes=64) for j in range(4)]
+        sums = keep.tile([P, 4, 2], F32, name="sums")
+        means = [keep.tile([P, 1], F32, name="mean_%d" % j) for j in range(4)]
+        scratch4 = [keep.tile([P, 2], F32, name="scr_%d" % j) for j in range(4)]
+
+        def turn_rows(rows_list, engines):
+            res = []
+            i = 0
+            for rows in rows_list:
+                grouped = new_grouped()
+                for b in range(2):
+                    bank = turn_block(rows[:, b, :].bitcast(F32))
+                    empty_block(engines[i], bank, grouped, b)
+                    i += 1
+                res.append(grouped)
+            return res
+
+        def unit_mm(q, j, aq):
+            bank = psum.tile([P, 512], F32, name="unit", tag="unit", bufs=4)
+            for part in range(2):
+                for g in range(PASSES):
+                    mx(bank[:, part * 256 : (part + 1) * 256], xq[g], slice(j * P, (j + 1) * P), aq[part], slice(g * 256, (g + 1) * 256), g == 0, g == 1)
+            return bank
+
+        def unit_square(bank):
+            sq = stage.tile([P, 512], F32, name="sq1", tag="sq1", bufs=4, align_bytes=64)
+            nc.scalar.activation(out=sq[:], in_=bank[:], func=ACT.Square)
+            return sq
+
+        def unit_view(q, j):
+            return u1[j][:, q // 2, :, (q % 2) * 128 : (q % 2) * 128 + 128]
+
+        def unit_add(q, j, sq):
+            a = sq[:, 0:256].rearrange("p (w u e) -> p u w e", u=2, e=2)
+            b = sq[:, 256:512].rearrange("p (w u e) -> p u w e", u=2, e=2)
+            nc.vector.tensor_tensor(out=unit_view(q, j).rearrange("p u (w e) -> p u w e", e=2), in0=a, in1=b, op=ALU.add)
+
+        def half_sqrt(g, j):
+            v = u1[j][:, g].rearrange("p u w -> p (u w)")
+            nc.scalar.activation(out=v, in_=v, func=ACT.Sqrt, bias=quarter[:], accum_out=sums[:, j, g : g + 1])
+
+        def centre(j):
+            nc.vector.tensor_scalar(out=scratch4[j][:], in0=sums[:, j, :], scalar1=1.0 / F, scalar2=None, op0=ALU.mult, op1=ALU.add, accum_out=means[j][:])
+            nc.vector.scalar_tensor_tensor(
+                out=n1[j][:].rearrange("p g u w -> p (g u w)"),
+                in0=u1[j][:].rearrange("p g u w -> p (g u w)"),
+                scalar=means[j][:],
+                in1=gain[:].rearrange("p g u w -> p (g u w)"),
+                op0=ALU.subtract,
+                op1=ALU.mult,
+            )
+
+        cr_wide = {}
+
+        def widen(b):
+            t = stage.tile([P, F], BF16, name="cr_wide", tag="cr_wide", bufs=4, align_bytes=64)
+            nc.vector.tensor_tensor(out=t[:], in0=cr_raw[b // 4][:, b % 4, :].bitcast(FP8), in1=scale[:], op=ALU.mult)
+            cr_wide[b] = t
+
+        gr = {}
+        gr[0] = turn_rows([a_rows[0, 0], a_rows[1, 0]], "SSSS")
+        aq = {0: [quantise_pair(t, "a", 8) for t in gr[0]]}
+        gr[1] = turn_rows([a_rows[0, 1], a_rows[1, 1]], "SSVV")
+        cim_rows = {p: load_pair(cim, p, False) for p in range(4)}
+        phi_rows = {p: load_pair(phi, p, False) for p in range(2)}
+        for q in range(4):
+            banks = [unit_mm(q, j, aq[q]) for j in range(4)]
+            aq[q + 1] = []
+            for j in range(4):
+                sq = unit_square(banks[j])
+                if j < 2:
+                    aq[q + 1].append(quantise_pair(gr[q + 1][j], "a" if q < 3 else "cim", 8 if q < 3 else 4))
+                unit_add(q, j, sq)
+            if q == 1:
+                for j in range(4):
+                    half_sqrt(0, j)
+            if q == 0:
+                gr[2] = turn_rows([a_rows[0, 2], a_rows[1, 2]], "SVSV")
+            elif q == 1:
+                gr[3] = turn_rows([a_rows[0, 3], a_rows[1, 3]], "VVVV")
+                spread_gain()
+            elif q == 2:
+                gr[4] = turn_rows([cim_rows[0], cim_rows[1]], "SSSS")
+                widen(0)
+                widen(1)
+        cimq = list(aq[4])
+
+        n_grouped = keep.tile([P, PASSES, C, 4], BF16, name="n_grouped", align_bytes=64)
+
+        def turn_n(j, engine):
+            bank = psum.tile([P, 4, P], F32, name="turned", tag="turned", bufs=4)
+            for g in range(PASSES):
+                for u in range(2):
+                    nc.tensor.transpose(bank[:, 2 * g + u, :], n1[j][:, g, u, :].bitcast(F32), ident[:])
+            dst = n_grouped[:].rearrange("p g n t -> p (g n t)").bitcast(F32).rearrange("p (g n u) -> p g n u", g=PASSES, u=2)[:, :, j * P : (j + 1) * P, :]
+            src = bank[:].rearrange("p (g u) n -> p g n u", u=2)
+            if engine == "S":
+                nc.scalar.copy(out=dst, in_=src)
+            else:
+                nc.vector.tensor_copy(out=dst, in_=src)
+
+        def turn_cr(pair, engines):
+            grouped = new_grouped()
+            for b in range(2):
+                bank = turn_block(cr_wide[2 * pair + b][:].bitcast(F32))
+                empty_block(engines[b], bank, grouped, b)
+            return grouped
+
+        def turn_pair(kind, pair, engines):
+            if kind == "cr":
+                return turn_cr(pair, engines)
+            return turn_rows([cim_rows[pair] if kind == "cim" else phi_rows[pair]], engines)[0]
+
+        ready = {"cr": [], "cim": cimq, "phi": []}
+        g_cr = turn_pair("cr", 0, "SS")
+        g_cim2 = turn_pair("cim", 2, "SS")
+        widen(2)
+        widen(3)
+        for j in range(4):
+            half_sqrt(1, j)
+            centre(j)
+        g_cr1 = turn_pair("cr", 1, "SS")
+        for j in range(4):
+            turn_n(j, "S")
+        ready["cr"].append(quantise_pair(g_cr, "cr", 4))
+        nq = [quantise(n_grouped[:, g].rearrange("p n t -> p (n t)"), "n", 2) for g in range(PASSES)]
+        g_cim3 = turn_pair("cim", 3, "SS")
+        ready["cr"].append(quantise_pair(g_cr1, "cr", 4))
+        ready["cim"].append(quantise_pair(g_cim2, "cim", 4))
+        widen(4)
+
+        def product(weights, m):
+            bank = psum.tile([P, 512], F32, name="unit", tag="unit", bufs=4)
+            lo = (m % 2) * P
+            for g in range(PASSES):
+                mx(bank[:], weights[m // 2], slice(g * 256 + lo, g * 256 + lo + P), nq[g], slice(0, C), g == 0, g == 1)
+            return bank
+
+        def first_order(t):
+            bank = product(ready["phi"], t)
+            res = stage.tile([P, C], F32, name="s1_out", tag="s1_out", bufs=2, align_bytes=64)
+            nc.vector.tensor_copy(out=res[:], in_=bank[:])
+            nc.sync.dma_start(out=out_0[t * P : (t + 1) * P, :], in_=res[:])
+
+        def finish(m, sq):
+            res = stage.tile([P, C], F32, name="u2_out", tag="u2_out", bufs=3, align_bytes=64)
+            nc.scalar.activation(out=res[:], in_=sq[:, 0, :], func=ACT.Sqrt, bias=quarter[:])
+            nc.sync.dma_start(out=out_1[m * P : (m + 1) * P, :], in_=res[:])
+
+        carried = [("phi", 0), ("cr", 2), ("phi", 1), ("cr", 3)]
+        waiting = ("cim", g_cim3)
+        prev = None
+        for m in range(8):
+            banks = [product(ready["cr"], m), product(ready["cim"], m)]
+            sq = stage.tile([P, 2, C], F32, name="sq2", tag="sq2", bufs=3, align_bytes=64)
+            for i in range(2):
+                nc.scalar.activation(out=sq[:, i, :], in_=banks[i][:], func=ACT.Square)
+            if m < 3:
+                widen(m + 5)
+            if waiting is not None:
+                ready[waiting[0]].append(quantise_pair(waiting[1], waiting[0], 2 if waiting[0] == "phi" else 4))
+                waiting = None
+            nc.vector.tensor_tensor(out=sq[:, 0, :], in0=sq[:, 0, :], in1=sq[:, 1, :], op=ALU.add)
+            if m < len(carried):
+                kind, pair = carried[m]
+                waiting = (kind, turn_pair(kind, pair, "SV" if m > 1 else "SS"))
+            if prev is not None:
+                finish(prev[0], prev[1])
+            prev = (m, sq)
+            if m in (2, 3, 5, 6):
+                first_order((2, 3, 5, 6).index(m))
+        finish(prev[0], prev[1])

@@ -4,6 +4,15 @@ import concourse.mybir as mybir
 from concourse.masks import make_identity
 
 S, F, G, T, C = 1024, 1024, 1024, 512, 512
+CFG = {'car': 0, 'fo': [2, 2, 5, 5], 'head': 6, 'clk0': 1, 'clk1': 1, 'clk2': 0, 'clkn': 1, 'xs': 512, 'widen': {'q11': [1, 2], 'q20': [], 'q21': [], 'c2': [4, 5], 'm0': [], 'm1': [6], 'm2': [7], 'q10': [], 'q01': [0], 'q31': [], 'q30': [], 'c0': [3]}}
+EX = 'SSSSSSSVSVSSVSVVSSSVSVSSSSSSSSSSSSSSSSVVVVVV'
+USED = []
+def pick(d):
+    i = len(USED)
+    e = d if EX is None else EX[i]
+    USED.append(e)
+    return e
+
 FLOPS = 2 * C * (2 * F * S + 2 * G * F + T * F)
 
 F32 = mybir.dt.float32
@@ -22,12 +31,17 @@ WORDS = 512
 
 def tile_learnedsecondorderscattering_kernel(tc, x, ar, aim, g1, cr_bytes, cr_scale, cim, phi, out_0, out_1):
     nc = tc.nc
+    USED.clear()
     with ExitStack() as ctx:
         keep = ctx.enter_context(tc.tile_pool(name="keep", bufs=1))
         stage = ctx.enter_context(tc.tile_pool(name="stage", bufs=1))
         psum = ctx.enter_context(tc.psum_pool(name="psum", bufs=1))
         ctx.enter_context(tc.manual_schedule())
 
+        cols_s = keep.tile([P, 8], F32, name="cols_s")
+        cols_g = keep.tile([P, 8], BF16, name="cols_g")
+        nc.scalar.dma_start(out=cols_s[:], in_=cr_scale.rearrange("o (n c) -> n (o c)", c=8))
+        nc.scalar.dma_start(out=cols_g[:], in_=g1.rearrange("(n c) -> n c", c=8))
         def load_pair(matrix, pair, split):
             rows = stage.tile([P, 2, S], BF16, name="rows", tag="rows", bufs=10, align_bytes=64)
             src = matrix[pair * 256 : (pair + 1) * 256, :].rearrange("(b p) k -> p b k", b=2)
@@ -48,10 +62,6 @@ def tile_learnedsecondorderscattering_kernel(tc, x, ar, aim, g1, cr_bytes, cr_sc
         for q in range(1, 4):
             a_rows[0, q] = load_pair(ar, q, q < 2)
             a_rows[1, q] = load_pair(aim, q, q < 2)
-        scale = keep.tile([P, F], F32, name="scale", align_bytes=64)
-        nc.sync.dma_start(out=scale[:], in_=cr_scale.rearrange("o k -> (o k)").partition_broadcast(P))
-        gain_flat = keep.tile([P, F], BF16, name="gain_flat", align_bytes=64)
-        nc.sync.dma_start(out=gain_flat[:], in_=g1.partition_broadcast(P))
         cr_raw = []
         for h in range(2):
             t = keep.tile([P, 4, F], U8, name="cr_raw%d" % h, align_bytes=64)
@@ -62,6 +72,8 @@ def tile_learnedsecondorderscattering_kernel(tc, x, ar, aim, g1, cr_bytes, cr_sc
         make_identity(nc, ident[:])
         quarter = keep.tile([P, 1], F32, name="quarter")
         nc.vector.memset(quarter[:], 0.25)
+        filler = keep.tile([P, C], BF16, name="filler", align_bytes=64)
+        nc.vector.memset(filler[:], 0.0)
         warm = keep.tile([P, 1], F32, name="warm")
         nc.scalar.activation(out=warm[:], in_=quarter[:], func=ACT.Sqrt)
 
@@ -76,6 +88,7 @@ def tile_learnedsecondorderscattering_kernel(tc, x, ar, aim, g1, cr_bytes, cr_sc
             return stage.tile([P, PASSES, QROWS, 4], BF16, name="grouped", tag="grouped", bufs=6, align_bytes=64)
 
         def empty_block(engine, bank, grouped, half):
+            engine = pick(engine)
             dst = grouped[:].rearrange("p g r t -> p (g r t)").bitcast(F32).rearrange("p (g r u) -> p g r u", g=PASSES, u=2)
             dst = dst[:, :, half * P : (half + 1) * P, :]
             src = bank[:].rearrange("p (g u) r -> p g r u", u=2)
@@ -105,19 +118,40 @@ def tile_learnedsecondorderscattering_kernel(tc, x, ar, aim, g1, cr_bytes, cr_sc
                 stop=stop,
             )
 
-        gain = keep.tile([P, PASSES, 2, 256], BF16, name="gain", align_bytes=64)
+        spread_s = keep.tile([P, 8, P], F32, name="spread_s", align_bytes=64)
+        spread_g = keep.tile([P, 8, P], F32, name="spread_g", align_bytes=64)
+        nc.vector.tensor_copy(out=spread_s[:], in_=cols_s[:].unsqueeze(2).to_broadcast([P, 8, P]))
+        nc.vector.tensor_copy(out=spread_g[:], in_=cols_g[:].unsqueeze(2).to_broadcast([P, 8, P]))
+        gain = keep.tile([P, PASSES, 2, 256], F32, name="gain", align_bytes=64)
+        scale = keep.tile([P, F], F32, name="scale", align_bytes=64)
 
-        def spread_gain():
-            for g in range(PASSES):
-                nc.vector.tensor_copy(
-                    out=gain[:, g].bitcast(F32),
-                    in_=gain_flat[:, g * 512 : (g + 1) * 512].bitcast(F32).rearrange("p (w u) -> p u w", u=2),
-                )
+        def spread_columns(spread, h):
+            bank = psum.tile([P, 4, P], F32, name="turned", tag="turned", bufs=4)
+            for i in range(4):
+                nc.tensor.transpose(bank[:, i, :], spread[:, 4 * h + i, :], ident[:])
+            return bank
+
+        def spread_constants():
+            for h in range(2):
+                bank = spread_columns(spread_s, h)
+                nc.scalar.copy(out=scale[:].rearrange("p (n c) -> p n c", c=8)[:, :, 4 * h : 4 * h + 4], in_=bank[:].rearrange("p c n -> p n c"))
+            for h in range(2):
+                bank = spread_columns(spread_g, h)
+                for g in range(PASSES):
+                    nc.scalar.copy(
+                        out=gain[:, g].rearrange("p u (n w e) -> p u n w e", w=2, e=2)[:, :, :, h, :],
+                        in_=bank[:].rearrange("p (u e) (g n) -> p g u n e", u=2, g=PASSES)[:, g],
+                    )
+
+        def keep_clock(n):
+            for i in range(n):
+                bank = psum.tile([P, 512], F32, name="unit", tag="unit", bufs=4)
+                nc.tensor.matmul(bank[:], lhsT=filler[:, 0:P], rhs=filler[:], start=True, stop=True)
 
         x_grouped = [stage.tile([P, C, 4], BF16, name="x_grouped", tag="x_grouped", bufs=2, align_bytes=64) for g in range(PASSES)]
         nc.vector.tensor_copy(out=x_grouped[0][:], in_=x_raw[0][:].rearrange("p t n -> p n t"))
-        nc.vector.tensor_copy(out=x_grouped[1][:], in_=x_raw[1][:].rearrange("p t n -> p n t"))
-        xq = [quantise(x_grouped[g][:].rearrange("p n t -> p (n t)"), "x", 2) for g in range(PASSES)]
+        nc.vector.tensor_copy(out=x_grouped[1][:, 0 : CFG["xs"], :], in_=x_raw[1][:, :, 0 : CFG["xs"]].rearrange("p t n -> p n t"))
+        xq = [quantise(x_grouped[0][:].rearrange("p n t -> p (n t)"), "x", 2)]
 
         u1 = [keep.tile([P, PASSES, 2, 256], F32, name="u1_%d" % j, align_bytes=64) for j in range(4)]
         n1 = [keep.tile([P, PASSES, 2, 256], BF16, name="n1_%d" % j, align_bytes=64) for j in range(4)]
@@ -162,7 +196,7 @@ def tile_learnedsecondorderscattering_kernel(tc, x, ar, aim, g1, cr_bytes, cr_sc
             nc.scalar.activation(out=v, in_=v, func=ACT.Sqrt, bias=quarter[:], accum_out=sums[:, j, g : g + 1])
 
         def centre(j):
-            nc.vector.tensor_scalar(out=scratch4[j][:], in0=sums[:, j, :], scalar1=1.0 / F, scalar2=None, op0=ALU.mult, op1=ALU.add, accum_out=means[j][:])
+            nc.scalar.activation(out=scratch4[j][:], in_=sums[:, j, :], func=ACT.Copy, scale=1.0 / F, accum_out=means[j][:])
             nc.vector.scalar_tensor_tensor(
                 out=n1[j][:].rearrange("p g u w -> p (g u w)"),
                 in0=u1[j][:].rearrange("p g u w -> p (g u w)"),
@@ -179,37 +213,52 @@ def tile_learnedsecondorderscattering_kernel(tc, x, ar, aim, g1, cr_bytes, cr_sc
             nc.vector.tensor_tensor(out=t[:], in0=cr_raw[b // 4][:, b % 4, :].bitcast(FP8), in1=scale[:], op=ALU.mult)
             cr_wide[b] = t
 
+        def hook(name):
+            for b in CFG["widen"].get(name, []):
+                widen(b)
+
         gr = {}
-        gr[0] = turn_rows([a_rows[0, 0], a_rows[1, 0]], "SSSS")
+        keep_clock(CFG["head"])
+        gr[0] = turn_rows([a_rows[0, 0]], "SS")
+        keep_clock(CFG["clk0"])
+        spread_constants()
+        if CFG["xs"] < 512:
+            nc.scalar.copy(out=x_grouped[1][:, CFG["xs"] : 512, :], in_=x_raw[1][:, :, CFG["xs"] : 512].rearrange("p t n -> p n t"))
+        xq.append(quantise(x_grouped[1][:].rearrange("p n t -> p (n t)"), "x", 2))
+        gr[0] += turn_rows([a_rows[1, 0]], "SS")
+        keep_clock(CFG["clk1"])
         aq = {0: [quantise_pair(t, "a", 8) for t in gr[0]]}
-        gr[1] = turn_rows([a_rows[0, 1], a_rows[1, 1]], "SSVV")
+        gr[1] = turn_rows([a_rows[0, 1]], "SS")
+        keep_clock(CFG["clk2"])
+        gr[1] += turn_rows([a_rows[1, 1]], "VV")
         cim_rows = {p: load_pair(cim, p, False) for p in range(4)}
         phi_rows = {p: load_pair(phi, p, False) for p in range(2)}
+        feed = {
+            0: ([a_rows[0, 2], a_rows[1, 2]], "SVSV"),
+            1: ([a_rows[0, 3], a_rows[1, 3]], "VVVV"),
+            2: ([cim_rows[0], cim_rows[1]], "SSSS"),
+        }
         for q in range(4):
-            banks = [unit_mm(q, j, aq[q]) for j in range(4)]
             aq[q + 1] = []
-            for j in range(4):
-                sq = unit_square(banks[j])
-                if j < 2:
-                    aq[q + 1].append(quantise_pair(gr[q + 1][j], "a" if q < 3 else "cim", 8 if q < 3 else 4))
-                unit_add(q, j, sq)
-            if q == 1:
-                for j in range(4):
-                    half_sqrt(0, j)
-            if q == 0:
-                gr[2] = turn_rows([a_rows[0, 2], a_rows[1, 2]], "SVSV")
-            elif q == 1:
-                gr[3] = turn_rows([a_rows[0, 3], a_rows[1, 3]], "VVVV")
-                spread_gain()
-            elif q == 2:
-                gr[4] = turn_rows([cim_rows[0], cim_rows[1]], "SSSS")
-                widen(0)
-                widen(1)
+            gr[q + 2] = []
+            for h in range(2):
+                banks = [unit_mm(q, j, aq[q]) for j in (2 * h, 2 * h + 1)]
+                sqs = [unit_square(bank) for bank in banks]
+                aq[q + 1].append(quantise_pair(gr[q + 1][h], "a" if q < 3 else "cim", 8 if q < 3 else 4))
+                for i in range(2):
+                    unit_add(q, 2 * h + i, sqs[i])
+                if q in feed:
+                    gr[q + 2] += turn_rows([feed[q][0][h]], feed[q][1][2 * h : 2 * h + 2])
+                hook("q%d%d" % (q, h))
+                if q == 1 and h == 1:
+                    for j in range(4):
+                        half_sqrt(0, j)
         cimq = list(aq[4])
 
         n_grouped = keep.tile([P, PASSES, C, 4], BF16, name="n_grouped", align_bytes=64)
 
         def turn_n(j, engine):
+            engine = pick(engine)
             bank = psum.tile([P, 4, P], F32, name="turned", tag="turned", bufs=4)
             for g in range(PASSES):
                 for u in range(2):
@@ -236,20 +285,21 @@ def tile_learnedsecondorderscattering_kernel(tc, x, ar, aim, g1, cr_bytes, cr_sc
         ready = {"cr": [], "cim": cimq, "phi": []}
         g_cr = turn_pair("cr", 0, "SS")
         g_cim2 = turn_pair("cim", 2, "SS")
-        widen(2)
-        widen(3)
+        hook("c0")
         for j in range(4):
             half_sqrt(1, j)
             centre(j)
         g_cr1 = turn_pair("cr", 1, "SS")
         for j in range(4):
             turn_n(j, "S")
+            keep_clock(CFG["clkn"])
+        hook("c1")
         ready["cr"].append(quantise_pair(g_cr, "cr", 4))
         nq = [quantise(n_grouped[:, g].rearrange("p n t -> p (n t)"), "n", 2) for g in range(PASSES)]
         g_cim3 = turn_pair("cim", 3, "SS")
         ready["cr"].append(quantise_pair(g_cr1, "cr", 4))
         ready["cim"].append(quantise_pair(g_cim2, "cim", 4))
-        widen(4)
+        hook("c2")
 
         def product(weights, m):
             bank = psum.tile([P, 512], F32, name="unit", tag="unit", bufs=4)
@@ -261,7 +311,7 @@ def tile_learnedsecondorderscattering_kernel(tc, x, ar, aim, g1, cr_bytes, cr_sc
         def first_order(t):
             bank = product(ready["phi"], t)
             res = stage.tile([P, C], F32, name="s1_out", tag="s1_out", bufs=2, align_bytes=64)
-            nc.vector.tensor_copy(out=res[:], in_=bank[:])
+            (nc.scalar.copy if pick("V") == "S" else nc.vector.tensor_copy)(out=res[:], in_=bank[:])
             nc.sync.dma_start(out=out_0[t * P : (t + 1) * P, :], in_=res[:])
 
         def finish(m, sq):
@@ -270,6 +320,8 @@ def tile_learnedsecondorderscattering_kernel(tc, x, ar, aim, g1, cr_bytes, cr_sc
             nc.sync.dma_start(out=out_1[m * P : (m + 1) * P, :], in_=res[:])
 
         carried = [("phi", 0), ("cr", 2), ("phi", 1), ("cr", 3)]
+        if CFG["car"]:
+            carried = [("cr", 2), ("phi", 0), ("cr", 3), ("phi", 1)]
         waiting = ("cim", g_cim3)
         prev = None
         for m in range(8):
@@ -277,8 +329,7 @@ def tile_learnedsecondorderscattering_kernel(tc, x, ar, aim, g1, cr_bytes, cr_sc
             sq = stage.tile([P, 2, C], F32, name="sq2", tag="sq2", bufs=3, align_bytes=64)
             for i in range(2):
                 nc.scalar.activation(out=sq[:, i, :], in_=banks[i][:], func=ACT.Square)
-            if m < 3:
-                widen(m + 5)
+            hook("m%d" % m)
             if waiting is not None:
                 ready[waiting[0]].append(quantise_pair(waiting[1], waiting[0], 2 if waiting[0] == "phi" else 4))
                 waiting = None
@@ -289,6 +340,7 @@ def tile_learnedsecondorderscattering_kernel(tc, x, ar, aim, g1, cr_bytes, cr_sc
             if prev is not None:
                 finish(prev[0], prev[1])
             prev = (m, sq)
-            if m in (2, 3, 5, 6):
-                first_order((2, 3, 5, 6).index(m))
+            for t in range(4):
+                if CFG["fo"][t] == m:
+                    first_order(t)
         finish(prev[0], prev[1])

@@ -4,8 +4,8 @@ import concourse.mybir as mybir
 from concourse.masks import make_identity
 
 S, F, G, T, C = 1024, 1024, 1024, 512, 512
-CFG = {'car': 0, 'fo': [2, 2, 5, 5], 'head': 6, 'clk0': 1, 'clk1': 1, 'clk2': 0, 'clkn': 1, 'xs': 512, 'widen': {'q11': [1, 2], 'q20': [], 'q21': [], 'c2': [4, 5], 'm0': [], 'm1': [6], 'm2': [7], 'q10': [], 'q01': [0], 'q31': [], 'q30': [], 'c0': [3]}}
-EX = 'SSSSSSSVSVSSVSVVSSSVSVSSSSSSSSSSSSSSSSVVVVVV'
+CFG = {'order': 0, 'split': 0, 'car': 0, 'fo': [2, 4, 5, 6], 'clkc': 2, 'head': 6, 'clk0': 2, 'clk1': 4, 'clk2': 1, 'clkn': 1, 'xs': 512, 'widen': {'q11': [0], 'q20': [], 'q21': [1], 'c2': [], 'm0': [5, 6], 'm1': [7], 'm2': [], 'q10': [2], 'c0': [], 'q01': [3], 'q30': [], 'm3': [], 'c1': [4], 'q31': []}}
+EX = 'SSSSSSVVSSVVVVSSVVSSSSVVSSSSSSSSSSSVSSVSVVVV'
 USED = []
 def pick(d):
     i = len(USED)
@@ -52,16 +52,24 @@ def tile_learnedsecondorderscattering_kernel(tc, x, ar, aim, g1, cr_bytes, cr_sc
                 nc.sync.dma_start(out=rows[:], in_=src)
             return rows
 
-        a_rows = {(0, 0): load_pair(ar, 0, True)}
-        x_raw = []
-        for g in range(PASSES):
-            t = keep.tile([P, 4, C], BF16, name="x_raw%d" % g, align_bytes=64)
-            nc.sync.dma_start(out=t[:], in_=x.rearrange("(g p t) n -> g p t n", p=P, t=4)[g])
-            x_raw.append(t)
-        a_rows[1, 0] = load_pair(aim, 0, True)
+        x_raw = {}
+        a_rows = {}
+
+        def load_x(g):
+            x_raw[g] = keep.tile([P, 4, C], BF16, name="x_raw%d" % g, align_bytes=64)
+            nc.sync.dma_start(out=x_raw[g][:], in_=x.rearrange("(g p t) n -> g p t n", p=P, t=4)[g])
+
+        def load_a(part, q):
+            a_rows[part, q] = load_pair((ar, aim)[part], q, q < 2)
+
+        for ch in ("a01b", "0a1b", "01ab")[CFG["order"]]:
+            if ch in "01":
+                load_x(int(ch))
+            else:
+                load_a("ab".index(ch), 0)
         for q in range(1, 4):
-            a_rows[0, q] = load_pair(ar, q, q < 2)
-            a_rows[1, q] = load_pair(aim, q, q < 2)
+            load_a(0, q)
+            load_a(1, q)
         cr_raw = []
         for h in range(2):
             t = keep.tile([P, 4, F], U8, name="cr_raw%d" % h, align_bytes=64)
@@ -136,11 +144,13 @@ def tile_learnedsecondorderscattering_kernel(tc, x, ar, aim, g1, cr_bytes, cr_sc
                 bank = spread_columns(spread_s, h)
                 nc.scalar.copy(out=scale[:].rearrange("p (n c) -> p n c", c=8)[:, :, 4 * h : 4 * h + 4], in_=bank[:].rearrange("p c n -> p n c"))
             for h in range(2):
-                bank = spread_columns(spread_g, h)
+                bank = psum.tile([P, 4, P], F32, name="turned", tag="turned", bufs=4)
+                for i in range(4):
+                    nc.tensor.transpose(bank[:, i, :], spread_g[:, 4 * (i // 2) + 2 * h + i % 2, :], ident[:])
                 for g in range(PASSES):
                     nc.scalar.copy(
-                        out=gain[:, g].rearrange("p u (n w e) -> p u n w e", w=2, e=2)[:, :, :, h, :],
-                        in_=bank[:].rearrange("p (u e) (g n) -> p g u n e", u=2, g=PASSES)[:, g],
+                        out=gain[:, g, h, :].rearrange("p (n z) -> p n z", z=4),
+                        in_=bank[:].rearrange("p z (g n) -> p g n z", g=PASSES)[:, g],
                     )
 
         def keep_clock(n):
@@ -217,43 +227,58 @@ def tile_learnedsecondorderscattering_kernel(tc, x, ar, aim, g1, cr_bytes, cr_sc
             for b in CFG["widen"].get(name, []):
                 widen(b)
 
-        gr = {}
+        seq = [("ar", 0), ("aim", 0), ("ar", 1), ("aim", 1), ("ar", 2), ("aim", 2), ("ar", 3), ("aim", 3), ("cim", 0), ("cim", 1), ("cr", 0)]
+        grouped_of = {}
+        ready = {"ar": [], "aim": [], "cim": [], "cr": [], "phi": []}
+        depth = {"ar": 4, "aim": 4, "cim": 4, "cr": 4, "phi": 2}
+        cim_rows = {}
+        phi_rows = {}
+
+        def turn(item, engines):
+            kind, pair = item
+            grouped = new_grouped()
+            for b in range(2):
+                if kind == "cr":
+                    words = cr_wide[2 * pair + b][:].bitcast(F32)
+                else:
+                    rows = {"ar": a_rows.get((0, pair)), "aim": a_rows.get((1, pair)), "cim": cim_rows.get(pair), "phi": phi_rows.get(pair)}[kind]
+                    words = rows[:, b, :].bitcast(F32)
+                empty_block(engines[b], turn_block(words), grouped, b)
+            grouped_of[item] = grouped
+
+        def pack(item):
+            ready[item[0]].append(quantise_pair(grouped_of[item], item[0], depth[item[0]]))
+
         keep_clock(CFG["head"])
-        gr[0] = turn_rows([a_rows[0, 0]], "SS")
+        turn(seq[0], "SS")
         keep_clock(CFG["clk0"])
         spread_constants()
         if CFG["xs"] < 512:
             nc.scalar.copy(out=x_grouped[1][:, CFG["xs"] : 512, :], in_=x_raw[1][:, :, CFG["xs"] : 512].rearrange("p t n -> p n t"))
         xq.append(quantise(x_grouped[1][:].rearrange("p n t -> p (n t)"), "x", 2))
-        gr[0] += turn_rows([a_rows[1, 0]], "SS")
+        turn(seq[1], "SS")
         keep_clock(CFG["clk1"])
-        aq = {0: [quantise_pair(t, "a", 8) for t in gr[0]]}
-        gr[1] = turn_rows([a_rows[0, 1]], "SS")
+        pack(seq[0])
+        pack(seq[1])
+        turn(seq[2], "SS")
         keep_clock(CFG["clk2"])
-        gr[1] += turn_rows([a_rows[1, 1]], "VV")
-        cim_rows = {p: load_pair(cim, p, False) for p in range(4)}
-        phi_rows = {p: load_pair(phi, p, False) for p in range(2)}
-        feed = {
-            0: ([a_rows[0, 2], a_rows[1, 2]], "SVSV"),
-            1: ([a_rows[0, 3], a_rows[1, 3]], "VVVV"),
-            2: ([cim_rows[0], cim_rows[1]], "SSSS"),
-        }
-        for q in range(4):
-            aq[q + 1] = []
-            gr[q + 2] = []
-            for h in range(2):
-                banks = [unit_mm(q, j, aq[q]) for j in (2 * h, 2 * h + 1)]
-                sqs = [unit_square(bank) for bank in banks]
-                aq[q + 1].append(quantise_pair(gr[q + 1][h], "a" if q < 3 else "cim", 8 if q < 3 else 4))
-                for i in range(2):
-                    unit_add(q, 2 * h + i, sqs[i])
-                if q in feed:
-                    gr[q + 2] += turn_rows([feed[q][0][h]], feed[q][1][2 * h : 2 * h + 2])
-                hook("q%d%d" % (q, h))
-                if q == 1 and h == 1:
-                    for j in range(4):
-                        half_sqrt(0, j)
-        cimq = list(aq[4])
+        for p in range(4):
+            cim_rows[p] = load_pair(cim, p, False)
+        for k in range(8):
+            q, h = k // 2, k % 2
+            banks = [unit_mm(q, j, (ready["ar"][q], ready["aim"][q])) for j in (2 * h, 2 * h + 1)]
+            sqs = [unit_square(bank) for bank in banks]
+            pack(seq[k + 2])
+            for i in range(2):
+                unit_add(q, 2 * h + i, sqs[i])
+            turn(seq[k + 3], "SV")
+            if k == 0:
+                for p in range(2):
+                    phi_rows[p] = load_pair(phi, p, False)
+            hook("q%d%d" % (q, h))
+            if k == 3:
+                for j in range(4):
+                    half_sqrt(0, j)
 
         n_grouped = keep.tile([P, PASSES, C, 4], BF16, name="n_grouped", align_bytes=64)
 
@@ -270,35 +295,24 @@ def tile_learnedsecondorderscattering_kernel(tc, x, ar, aim, g1, cr_bytes, cr_sc
             else:
                 nc.vector.tensor_copy(out=dst, in_=src)
 
-        def turn_cr(pair, engines):
-            grouped = new_grouped()
-            for b in range(2):
-                bank = turn_block(cr_wide[2 * pair + b][:].bitcast(F32))
-                empty_block(engines[b], bank, grouped, b)
-            return grouped
-
-        def turn_pair(kind, pair, engines):
-            if kind == "cr":
-                return turn_cr(pair, engines)
-            return turn_rows([cim_rows[pair] if kind == "cim" else phi_rows[pair]], engines)[0]
-
-        ready = {"cr": [], "cim": cimq, "phi": []}
-        g_cr = turn_pair("cr", 0, "SS")
-        g_cim2 = turn_pair("cim", 2, "SS")
+        turn(("cim", 2), "SS")
+        keep_clock(CFG["clkc"])
         hook("c0")
         for j in range(4):
             half_sqrt(1, j)
             centre(j)
-        g_cr1 = turn_pair("cr", 1, "SS")
+        turn(("cr", 1), "SS")
+        keep_clock(CFG["clkc"])
         for j in range(4):
             turn_n(j, "S")
             keep_clock(CFG["clkn"])
         hook("c1")
-        ready["cr"].append(quantise_pair(g_cr, "cr", 4))
+        pack(("cr", 0))
         nq = [quantise(n_grouped[:, g].rearrange("p n t -> p (n t)"), "n", 2) for g in range(PASSES)]
-        g_cim3 = turn_pair("cim", 3, "SS")
-        ready["cr"].append(quantise_pair(g_cr1, "cr", 4))
-        ready["cim"].append(quantise_pair(g_cim2, "cim", 4))
+        turn(("cim", 3), "SS")
+        keep_clock(CFG["clkc"])
+        pack(("cr", 1))
+        pack(("cim", 2))
         hook("c2")
 
         def product(weights, m):
@@ -322,25 +336,40 @@ def tile_learnedsecondorderscattering_kernel(tc, x, ar, aim, g1, cr_bytes, cr_sc
         carried = [("phi", 0), ("cr", 2), ("phi", 1), ("cr", 3)]
         if CFG["car"]:
             carried = [("cr", 2), ("phi", 0), ("cr", 3), ("phi", 1)]
-        waiting = ("cim", g_cim3)
+        waiting = ("cim", 3)
         prev = None
         for m in range(8):
             banks = [product(ready["cr"], m), product(ready["cim"], m)]
+            if m == 7 and CFG["split"]:
+                finish(prev[0], prev[1])
+                sq = stage.tile([P, 2, C], F32, name="sq2", tag="sq2", bufs=3, align_bytes=64)
+                res = stage.tile([P, C], F32, name="u2_out", tag="u2_out", bufs=3, align_bytes=64)
+                for z in range(2):
+                    cols = slice(256 * z, 256 * z + 256)
+                    for i in range(2):
+                        nc.scalar.activation(out=sq[:, i, cols], in_=banks[i][:, cols], func=ACT.Square)
+                    nc.vector.tensor_tensor(out=sq[:, 0, cols], in0=sq[:, 0, cols], in1=sq[:, 1, cols], op=ALU.add)
+                for z in range(2):
+                    cols = slice(256 * z, 256 * z + 256)
+                    nc.scalar.activation(out=res[:, cols], in_=sq[:, 0, cols], func=ACT.Sqrt, bias=quarter[:])
+                    nc.sync.dma_start(out=out_1[m * P : (m + 1) * P, cols], in_=res[:, cols])
+                break
             sq = stage.tile([P, 2, C], F32, name="sq2", tag="sq2", bufs=3, align_bytes=64)
             for i in range(2):
                 nc.scalar.activation(out=sq[:, i, :], in_=banks[i][:], func=ACT.Square)
             hook("m%d" % m)
             if waiting is not None:
-                ready[waiting[0]].append(quantise_pair(waiting[1], waiting[0], 2 if waiting[0] == "phi" else 4))
+                pack(waiting)
                 waiting = None
             nc.vector.tensor_tensor(out=sq[:, 0, :], in0=sq[:, 0, :], in1=sq[:, 1, :], op=ALU.add)
             if m < len(carried):
-                kind, pair = carried[m]
-                waiting = (kind, turn_pair(kind, pair, "SV" if m > 1 else "SS"))
+                turn(carried[m], "SS")
+                waiting = carried[m]
             if prev is not None:
                 finish(prev[0], prev[1])
             prev = (m, sq)
             for t in range(4):
-                if CFG["fo"][t] == m:
+                if CFG["fo"][t] == m or (m == 6 and CFG["fo"][t] == 7):
                     first_order(t)
-        finish(prev[0], prev[1])
+        if not CFG["split"]:
+            finish(prev[0], prev[1])

@@ -4,15 +4,6 @@ import concourse.mybir as mybir
 from concourse.masks import make_identity
 
 S, F, G, T, C = 1024, 1024, 1024, 512, 512
-CFG = {'order': 0, 'split': 0, 'car': 0, 'fo': [2, 4, 5, 6], 'clkc': 2, 'head': 6, 'clk0': 2, 'clk1': 4, 'clk2': 1, 'clkn': 1, 'xs': 512, 'widen': {'q11': [0], 'q20': [], 'q21': [1], 'c2': [], 'm0': [5, 6], 'm1': [7], 'm2': [], 'q10': [2], 'c0': [], 'q01': [3], 'q30': [], 'm3': [], 'c1': [4], 'q31': []}}
-EX = 'SSSSSSVVSSVVVVSSVVSSSSVVSSSSSSSSSSSVSSVSVVVV'
-USED = []
-def pick(d):
-    i = len(USED)
-    e = d if EX is None else EX[i]
-    USED.append(e)
-    return e
-
 FLOPS = 2 * C * (2 * F * S + 2 * G * F + T * F)
 
 F32 = mybir.dt.float32
@@ -23,353 +14,312 @@ FP8 = mybir.dt.float8_e4m3fn
 FP8X4 = mybir.dt.float8_e4m3fn_x4
 ACT = mybir.ActivationFunctionType
 ALU = mybir.AluOpType
+
 P = 128
+PACK = 4
 PASSES = 2
-QROWS = 256
-WORDS = 512
+K_PASS = P * PACK
+PAIR = 2 * P
+BANK = 512
+COLUMN_TILES = C // P
+QUARTERS = F // PAIR
+
+WEIGHT_PAIRS = (
+    ("ar", 0, "SS"),
+    ("aim", 0, "SS"),
+    ("ar", 1, "SS"),
+    ("aim", 1, "SS"),
+    ("ar", 2, "SS"),
+    ("aim", 2, "VS"),
+    ("ar", 3, "VV"),
+    ("aim", 3, "SS"),
+    ("cim", 0, "SS"),
+    ("cim", 1, "SS"),
+    ("cr", 0, "VS"),
+    ("cim", 2, "VV"),
+    ("cr", 1, "SS"),
+    ("cim", 3, "SS"),
+    ("phi", 0, "SV"),
+    ("cr", 2, "SS"),
+    ("phi", 1, "VV"),
+    ("cr", 3, "SS"),
+)
+HEAD_PAIRS = 3
+STAGE1_PAIRS = 6
+SCALE_BEHIND_STAGE1 = {1: (2,), 3: (1, 5), 5: (3, 4)}
+SCALE_WITHIN_STAGE2 = {1: (6,)}
+FIRST_ORDER_BEHIND = {3: (0,), 4: (1,), 6: (2, 3)}
 
 
 def tile_learnedsecondorderscattering_kernel(tc, x, ar, aim, g1, cr_bytes, cr_scale, cim, phi, out_0, out_1):
     nc = tc.nc
-    USED.clear()
     with ExitStack() as ctx:
         keep = ctx.enter_context(tc.tile_pool(name="keep", bufs=1))
         stage = ctx.enter_context(tc.tile_pool(name="stage", bufs=1))
         psum = ctx.enter_context(tc.psum_pool(name="psum", bufs=1))
         ctx.enter_context(tc.manual_schedule())
 
-        cols_s = keep.tile([P, 8], F32, name="cols_s")
-        cols_g = keep.tile([P, 8], BF16, name="cols_g")
-        nc.scalar.dma_start(out=cols_s[:], in_=cr_scale.rearrange("o (n c) -> n (o c)", c=8))
-        nc.scalar.dma_start(out=cols_g[:], in_=g1.rearrange("(n c) -> n c", c=8))
-        def load_pair(matrix, pair, split):
-            rows = stage.tile([P, 2, S], BF16, name="rows", tag="rows", bufs=10, align_bytes=64)
-            src = matrix[pair * 256 : (pair + 1) * 256, :].rearrange("(b p) k -> p b k", b=2)
-            if split:
-                for b in range(2):
-                    nc.sync.dma_start(out=rows[:, b, :], in_=src[:, b, :])
-            else:
-                nc.sync.dma_start(out=rows[:], in_=src)
-            return rows
+        scale_cols = keep.tile([P, 8], F32, name="scale_cols")
+        gain_cols = keep.tile([P, 8], BF16, name="gain_cols")
+        nc.scalar.dma_start(out=scale_cols[:], in_=cr_scale.rearrange("o (n c) -> n (o c)", c=8))
+        nc.scalar.dma_start(out=gain_cols[:], in_=g1.rearrange("(n c) -> n c", c=8))
 
-        x_raw = {}
-        a_rows = {}
+        x_rows = {}
+        weight_rows = {}
+        cr_codes = {}
 
         def load_x(g):
-            x_raw[g] = keep.tile([P, 4, C], BF16, name="x_raw%d" % g, align_bytes=64)
-            nc.sync.dma_start(out=x_raw[g][:], in_=x.rearrange("(g p t) n -> g p t n", p=P, t=4)[g])
+            x_rows[g] = keep.tile([P, PACK, C], BF16, name="x_rows%d" % g, align_bytes=64)
+            nc.sync.dma_start(out=x_rows[g][:], in_=x.rearrange("(g p t) n -> g p t n", p=P, t=PACK)[g])
 
-        def load_a(part, q):
-            a_rows[part, q] = load_pair((ar, aim)[part], q, q < 2)
-
-        for ch in ("a01b", "0a1b", "01ab")[CFG["order"]]:
-            if ch in "01":
-                load_x(int(ch))
+        def load_pair(kind, pair, by_block):
+            matrix = {"ar": ar, "aim": aim, "cim": cim, "phi": phi}[kind]
+            rows = stage.tile([P, 2, S], BF16, name="rows", tag="rows", bufs=10, align_bytes=64)
+            source = matrix[pair * PAIR : (pair + 1) * PAIR, :].rearrange("(b p) k -> p b k", b=2)
+            if by_block:
+                for b in range(2):
+                    nc.sync.dma_start(out=rows[:, b, :], in_=source[:, b, :])
             else:
-                load_a("ab".index(ch), 0)
-        for q in range(1, 4):
-            load_a(0, q)
-            load_a(1, q)
-        cr_raw = []
-        for h in range(2):
-            t = keep.tile([P, 4, F], U8, name="cr_raw%d" % h, align_bytes=64)
-            nc.sync.dma_start(out=t[:], in_=cr_bytes[h * 512 : (h + 1) * 512, :].rearrange("(b p) k -> p b k", b=4))
-            cr_raw.append(t)
+                nc.sync.dma_start(out=rows[:], in_=source)
+            weight_rows[kind, pair] = rows
 
-        ident = keep.tile([P, P], F32, name="ident", align_bytes=64)
-        make_identity(nc, ident[:])
+        def load_cr(half):
+            cr_codes[half] = keep.tile([P, 4, F], U8, name="cr_codes%d" % half, align_bytes=64)
+            source = cr_bytes[half * 4 * P : (half + 1) * 4 * P, :].rearrange("(b p) k -> p b k", b=4)
+            nc.sync.dma_start(out=cr_codes[half][:], in_=source)
+
+        load_x(0)
+        load_pair("ar", 0, True)
+        load_x(1)
+        load_pair("aim", 0, True)
+        for q in range(1, QUARTERS):
+            load_pair("ar", q, q < 2)
+            load_pair("aim", q, q < 2)
+            if q < 3:
+                load_cr(q - 1)
+
+        identity = keep.tile([P, P], F32, name="identity", align_bytes=64)
+        make_identity(nc, identity[:])
         quarter = keep.tile([P, 1], F32, name="quarter")
         nc.vector.memset(quarter[:], 0.25)
         filler = keep.tile([P, C], BF16, name="filler", align_bytes=64)
         nc.vector.memset(filler[:], 0.0)
-        warm = keep.tile([P, 1], F32, name="warm")
-        nc.scalar.activation(out=warm[:], in_=quarter[:], func=ACT.Sqrt)
+        first_root = keep.tile([P, 1], F32, name="first_root")
+        nc.scalar.activation(out=first_root[:], in_=quarter[:], func=ACT.Sqrt)
+        scale_spread = stage.tile([P, 8, P], F32, name="scale_spread", tag="squares2", bufs=4, align_bytes=64)
+        gain_spread = stage.tile([P, 8, P], F32, name="gain_spread", tag="squares2", bufs=4, align_bytes=64)
+        nc.vector.tensor_copy(out=scale_spread[:], in_=scale_cols[:].unsqueeze(2).to_broadcast([P, 8, P]))
+        nc.vector.tensor_copy(out=gain_spread[:], in_=gain_cols[:].unsqueeze(2).to_broadcast([P, 8, P]))
+        gain = keep.tile([P, F], F32, name="gain", align_bytes=64)
+        scale = keep.tile([P, F], F32, name="scale", align_bytes=64)
 
-        def turn_block(words):
-            bank = psum.tile([P, 4, P], F32, name="turned", tag="turned", bufs=4)
+        def product_bank():
+            return psum.tile([P, BANK], F32, name="product", tag="product", bufs=4)
+
+        def transpose_bank():
+            return psum.tile([P, 4, P], F32, name="turned", tag="turned", bufs=4)
+
+        def hold_clock(n):
+            for i in range(n):
+                bank = product_bank()
+                nc.tensor.matmul(bank[:], lhsT=filler[:, 0:P], rhs=filler[:], start=True, stop=True)
+
+        def copy_out(engine, out, in_):
+            if engine == "S":
+                nc.scalar.copy(out=out, in_=in_)
+            else:
+                nc.vector.tensor_copy(out=out, in_=in_)
+
+        def transpose_rows(words):
+            bank = transpose_bank()
             for g in range(PASSES):
                 for u in range(2):
-                    nc.tensor.transpose(bank[:, 2 * g + u, :], words[:, 256 * g + u : 256 * (g + 1) : 2], ident[:])
+                    nc.tensor.transpose(bank[:, 2 * g + u, :], words[:, 256 * g + u : 256 * (g + 1) : 2], identity[:])
             return bank
 
-        def new_grouped():
-            return stage.tile([P, PASSES, QROWS, 4], BF16, name="grouped", tag="grouped", bufs=6, align_bytes=64)
-
-        def empty_block(engine, bank, grouped, half):
-            engine = pick(engine)
-            dst = grouped[:].rearrange("p g r t -> p (g r t)").bitcast(F32).rearrange("p (g r u) -> p g r u", g=PASSES, u=2)
-            dst = dst[:, :, half * P : (half + 1) * P, :]
-            src = bank[:].rearrange("p (g u) r -> p g r u", u=2)
-            if engine == "S":
-                nc.scalar.copy(out=dst, in_=src)
-            else:
-                nc.vector.tensor_copy(out=dst, in_=src)
+        def interleaved(grouped, first, width):
+            words = grouped[:].rearrange("p g r t -> p (g r t)").bitcast(F32)
+            words = words.rearrange("p (g r u) -> p g r u", g=PASSES, u=2)
+            return words[:, :, first : first + width, :]
 
         def quantise(flat, tag, bufs):
-            width = flat.shape[1] // 4
-            codes = keep.tile([P, width], U32, name="codes", tag=tag + "_c", bufs=bufs, align_bytes=64)
-            scales = keep.tile([P, width], U8, name="scales", tag=tag + "_s", bufs=bufs, align_bytes=64)
+            width = flat.shape[1] // PACK
+            codes = keep.tile([P, width], U32, name="codes", tag=tag + "_codes", bufs=bufs, align_bytes=64)
+            scales = keep.tile([P, width], U8, name="scales", tag=tag + "_scales", bufs=bufs, align_bytes=64)
             nc.vector.quantize_mx(out=codes[:].bitcast(FP8X4), scales=scales[:], in_=flat)
             return codes, scales
 
-        def quantise_pair(grouped, tag, bufs):
-            return quantise(grouped[:].rearrange("p g r t -> p (g r t)"), tag, bufs)
-
-        def mx(out, lhs, lcols, rhs, rcols, start, stop):
+        def mx(out, left, left_cols, right, right_cols, g):
             nc.tensor.matmul_mx(
                 out=out,
-                lhsT=lhs[0][:, lcols].bitcast(FP8X4),
-                lhsT_scale=lhs[1][:, lcols],
-                rhs=rhs[0][:, rcols].bitcast(FP8X4),
-                rhs_scale=rhs[1][:, rcols],
-                start=start,
-                stop=stop,
+                lhsT=left[0][:, left_cols].bitcast(FP8X4),
+                lhsT_scale=left[1][:, left_cols],
+                rhs=right[0][:, right_cols].bitcast(FP8X4),
+                rhs_scale=right[1][:, right_cols],
+                start=g == 0,
+                stop=g == PASSES - 1,
             )
 
-        spread_s = keep.tile([P, 8, P], F32, name="spread_s", align_bytes=64)
-        spread_g = keep.tile([P, 8, P], F32, name="spread_g", align_bytes=64)
-        nc.vector.tensor_copy(out=spread_s[:], in_=cols_s[:].unsqueeze(2).to_broadcast([P, 8, P]))
-        nc.vector.tensor_copy(out=spread_g[:], in_=cols_g[:].unsqueeze(2).to_broadcast([P, 8, P]))
-        gain = keep.tile([P, PASSES, 2, 256], F32, name="gain", align_bytes=64)
-        scale = keep.tile([P, F], F32, name="scale", align_bytes=64)
+        cr_scaled = {}
 
-        def spread_columns(spread, h):
-            bank = psum.tile([P, 4, P], F32, name="turned", tag="turned", bufs=4)
-            for i in range(4):
-                nc.tensor.transpose(bank[:, i, :], spread[:, 4 * h + i, :], ident[:])
-            return bank
+        def scale_cr(block):
+            rows = stage.tile([P, F], BF16, name="cr_scaled", tag="cr_scaled", bufs=8, align_bytes=64)
+            codes = cr_codes[block // 4][:, block % 4, :]
+            nc.vector.tensor_tensor(out=rows[:], in0=codes.bitcast(FP8), in1=scale[:], op=ALU.mult)
+            cr_scaled[block] = rows
 
-        def spread_constants():
-            for h in range(2):
-                bank = spread_columns(spread_s, h)
-                nc.scalar.copy(out=scale[:].rearrange("p (n c) -> p n c", c=8)[:, :, 4 * h : 4 * h + 4], in_=bank[:].rearrange("p c n -> p n c"))
-            for h in range(2):
-                bank = psum.tile([P, 4, P], F32, name="turned", tag="turned", bufs=4)
-                for i in range(4):
-                    nc.tensor.transpose(bank[:, i, :], spread_g[:, 4 * (i // 2) + 2 * h + i % 2, :], ident[:])
-                for g in range(PASSES):
-                    nc.scalar.copy(
-                        out=gain[:, g, h, :].rearrange("p (n z) -> p n z", z=4),
-                        in_=bank[:].rearrange("p z (g n) -> p g n z", g=PASSES)[:, g],
-                    )
+        pairs_to_turn = list(WEIGHT_PAIRS)
+        turned = {}
+        packed = {}
+        packed_bufs = {"ar": 4, "aim": 4, "cim": 4, "cr": 4, "phi": 2}
 
-        def keep_clock(n):
-            for i in range(n):
-                bank = psum.tile([P, 512], F32, name="unit", tag="unit", bufs=4)
-                nc.tensor.matmul(bank[:], lhsT=filler[:, 0:P], rhs=filler[:], start=True, stop=True)
-
-        x_grouped = [stage.tile([P, C, 4], BF16, name="x_grouped", tag="x_grouped", bufs=2, align_bytes=64) for g in range(PASSES)]
-        nc.vector.tensor_copy(out=x_grouped[0][:], in_=x_raw[0][:].rearrange("p t n -> p n t"))
-        nc.vector.tensor_copy(out=x_grouped[1][:, 0 : CFG["xs"], :], in_=x_raw[1][:, :, 0 : CFG["xs"]].rearrange("p t n -> p n t"))
-        xq = [quantise(x_grouped[0][:].rearrange("p n t -> p (n t)"), "x", 2)]
-
-        u1 = [keep.tile([P, PASSES, 2, 256], F32, name="u1_%d" % j, align_bytes=64) for j in range(4)]
-        n1 = [keep.tile([P, PASSES, 2, 256], BF16, name="n1_%d" % j, align_bytes=64) for j in range(4)]
-        sums = keep.tile([P, 4, 2], F32, name="sums")
-        means = [keep.tile([P, 1], F32, name="mean_%d" % j) for j in range(4)]
-        scratch4 = [keep.tile([P, 2], F32, name="scr_%d" % j) for j in range(4)]
-
-        def turn_rows(rows_list, engines):
-            res = []
-            i = 0
-            for rows in rows_list:
-                grouped = new_grouped()
-                for b in range(2):
-                    bank = turn_block(rows[:, b, :].bitcast(F32))
-                    empty_block(engines[i], bank, grouped, b)
-                    i += 1
-                res.append(grouped)
-            return res
-
-        def unit_mm(q, j, aq):
-            bank = psum.tile([P, 512], F32, name="unit", tag="unit", bufs=4)
-            for part in range(2):
-                for g in range(PASSES):
-                    mx(bank[:, part * 256 : (part + 1) * 256], xq[g], slice(j * P, (j + 1) * P), aq[part], slice(g * 256, (g + 1) * 256), g == 0, g == 1)
-            return bank
-
-        def unit_square(bank):
-            sq = stage.tile([P, 512], F32, name="sq1", tag="sq1", bufs=4, align_bytes=64)
-            nc.scalar.activation(out=sq[:], in_=bank[:], func=ACT.Square)
-            return sq
-
-        def unit_view(q, j):
-            return u1[j][:, q // 2, :, (q % 2) * 128 : (q % 2) * 128 + 128]
-
-        def unit_add(q, j, sq):
-            a = sq[:, 0:256].rearrange("p (w u e) -> p u w e", u=2, e=2)
-            b = sq[:, 256:512].rearrange("p (w u e) -> p u w e", u=2, e=2)
-            nc.vector.tensor_tensor(out=unit_view(q, j).rearrange("p u (w e) -> p u w e", e=2), in0=a, in1=b, op=ALU.add)
-
-        def half_sqrt(g, j):
-            v = u1[j][:, g].rearrange("p u w -> p (u w)")
-            nc.scalar.activation(out=v, in_=v, func=ACT.Sqrt, bias=quarter[:], accum_out=sums[:, j, g : g + 1])
-
-        def centre(j):
-            nc.scalar.activation(out=scratch4[j][:], in_=sums[:, j, :], func=ACT.Copy, scale=1.0 / F, accum_out=means[j][:])
-            nc.vector.scalar_tensor_tensor(
-                out=n1[j][:].rearrange("p g u w -> p (g u w)"),
-                in0=u1[j][:].rearrange("p g u w -> p (g u w)"),
-                scalar=means[j][:],
-                in1=gain[:].rearrange("p g u w -> p (g u w)"),
-                op0=ALU.subtract,
-                op1=ALU.mult,
-            )
-
-        cr_wide = {}
-
-        def widen(b):
-            t = stage.tile([P, F], BF16, name="cr_wide", tag="cr_wide", bufs=4, align_bytes=64)
-            nc.vector.tensor_tensor(out=t[:], in0=cr_raw[b // 4][:, b % 4, :].bitcast(FP8), in1=scale[:], op=ALU.mult)
-            cr_wide[b] = t
-
-        def hook(name):
-            for b in CFG["widen"].get(name, []):
-                widen(b)
-
-        seq = [("ar", 0), ("aim", 0), ("ar", 1), ("aim", 1), ("ar", 2), ("aim", 2), ("ar", 3), ("aim", 3), ("cim", 0), ("cim", 1), ("cr", 0)]
-        grouped_of = {}
-        ready = {"ar": [], "aim": [], "cim": [], "cr": [], "phi": []}
-        depth = {"ar": 4, "aim": 4, "cim": 4, "cr": 4, "phi": 2}
-        cim_rows = {}
-        phi_rows = {}
-
-        def turn(item, engines):
-            kind, pair = item
-            grouped = new_grouped()
+        def turn_next():
+            kind, pair, engines = pairs_to_turn[0]
+            pairs_to_turn.remove(pairs_to_turn[0])
+            grouped = stage.tile([P, PASSES, PAIR, PACK], BF16, name="grouped", tag="grouped", bufs=6, align_bytes=64)
             for b in range(2):
-                if kind == "cr":
-                    words = cr_wide[2 * pair + b][:].bitcast(F32)
-                else:
-                    rows = {"ar": a_rows.get((0, pair)), "aim": a_rows.get((1, pair)), "cim": cim_rows.get(pair), "phi": phi_rows.get(pair)}[kind]
-                    words = rows[:, b, :].bitcast(F32)
-                empty_block(engines[b], turn_block(words), grouped, b)
-            grouped_of[item] = grouped
+                block = cr_scaled[2 * pair + b][:] if kind == "cr" else weight_rows[kind, pair][:, b, :]
+                bank = transpose_rows(block.bitcast(F32))
+                copy_out(engines[b], interleaved(grouped, b * P, P), bank[:].rearrange("p (g u) r -> p g r u", u=2))
+            turned[kind, pair] = grouped
 
-        def pack(item):
-            ready[item[0]].append(quantise_pair(grouped_of[item], item[0], depth[item[0]]))
+        def pack(kind, pair):
+            packed[kind, pair] = quantise(turned[kind, pair][:].rearrange("p g r t -> p (g r t)"), kind, packed_bufs[kind])
 
-        keep_clock(CFG["head"])
-        turn(seq[0], "SS")
-        keep_clock(CFG["clk0"])
-        spread_constants()
-        if CFG["xs"] < 512:
-            nc.scalar.copy(out=x_grouped[1][:, CFG["xs"] : 512, :], in_=x_raw[1][:, :, CFG["xs"] : 512].rearrange("p t n -> p n t"))
-        xq.append(quantise(x_grouped[1][:].rearrange("p n t -> p (n t)"), "x", 2))
-        turn(seq[1], "SS")
-        keep_clock(CFG["clk1"])
-        pack(seq[0])
-        pack(seq[1])
-        turn(seq[2], "SS")
-        keep_clock(CFG["clk2"])
-        for p in range(4):
-            cim_rows[p] = load_pair(cim, p, False)
-        for k in range(8):
-            q, h = k // 2, k % 2
-            banks = [unit_mm(q, j, (ready["ar"][q], ready["aim"][q])) for j in (2 * h, 2 * h + 1)]
-            sqs = [unit_square(bank) for bank in banks]
-            pack(seq[k + 2])
+        hold_clock(1)
+        for spread, vector in ((scale_spread, scale), (gain_spread, gain)):
+            for half in range(2):
+                bank = transpose_bank()
+                for i in range(4):
+                    nc.tensor.transpose(bank[:, i, :], spread[:, 4 * half + i, :], identity[:])
+                columns = vector[:].rearrange("p (n c) -> p n c", c=8)[:, :, 4 * half : 4 * half + 4]
+                nc.scalar.copy(out=columns, in_=bank[:].rearrange("p c n -> p n c"))
+
+        x_grouped = []
+        for g in range(PASSES):
+            grouped = stage.tile([P, C, PACK], BF16, name="x_grouped", tag="x_grouped", bufs=2, align_bytes=64)
+            nc.vector.tensor_copy(
+                out=grouped[:].rearrange("p (c i) t -> p c t i", i=4),
+                in_=x_rows[g][:].rearrange("p t (c i) -> p c t i", i=4),
+            )
+            x_grouped.append(grouped)
+        x_packed = [quantise(grouped[:].rearrange("p n t -> p (n t)"), "x", 2) for grouped in x_grouped]
+
+        turn_next()
+        turn_next()
+        hold_clock(2)
+        pack("ar", 0)
+        pack("aim", 0)
+        scale_cr(0)
+        turn_next()
+        for pair in range(4):
+            load_pair("cim", pair, False)
+
+        u1 = keep.tile([P, COLUMN_TILES, F], F32, name="u1", align_bytes=64)
+        n1 = [keep.tile([P, F], BF16, name="n1_%d" % j, align_bytes=64) for j in range(COLUMN_TILES)]
+        sums = keep.tile([P, COLUMN_TILES, 2], F32, name="sums")
+        totals = [keep.tile([P, 1], F32, name="total_%d" % j) for j in range(COLUMN_TILES)]
+        means = [keep.tile([P, 1], F32, name="mean_%d" % j) for j in range(COLUMN_TILES)]
+
+        def root_half(half, j):
+            view = u1[:, j, F // 2 * half : F // 2 * (half + 1)]
+            nc.scalar.activation(out=view, in_=view, func=ACT.Sqrt, bias=quarter[:], accum_out=sums[:, j, half : half + 1])
+
+        for step in range(2 * QUARTERS):
+            q, side = step // 2, step % 2
+            banks = []
+            for j in (2 * side, 2 * side + 1):
+                bank = product_bank()
+                for part, kind in enumerate(("ar", "aim")):
+                    for g in range(PASSES):
+                        f_cols = slice(PAIR * g, PAIR * (g + 1))
+                        mx(bank[:, PAIR * part : PAIR * (part + 1)], x_packed[g], slice(P * j, P * (j + 1)), packed[kind, q], f_cols, g)
+                banks.append(bank)
+            squares = stage.tile([P, 2, BANK], F32, name="squares", tag="squares2", bufs=4, align_bytes=64)
             for i in range(2):
-                unit_add(q, 2 * h + i, sqs[i])
-            turn(seq[k + 3], "SV")
-            if k == 0:
-                for p in range(2):
-                    phi_rows[p] = load_pair(phi, p, False)
-            hook("q%d%d" % (q, h))
-            if k == 3:
-                for j in range(4):
-                    half_sqrt(0, j)
+                nc.scalar.activation(out=squares[:, i, :], in_=banks[i][:], func=ACT.Square)
+            if step < STAGE1_PAIRS + 1:
+                pack(WEIGHT_PAIRS[step + 2][0], WEIGHT_PAIRS[step + 2][1])
+            nc.vector.tensor_tensor(
+                out=u1[:, 2 * side : 2 * side + 2, PAIR * q : PAIR * (q + 1)],
+                in0=squares[:, :, 0:PAIR],
+                in1=squares[:, :, PAIR : 2 * PAIR],
+                op=ALU.add,
+            )
+            if step < STAGE1_PAIRS:
+                turn_next()
+            if step == 0:
+                for pair in range(2):
+                    load_pair("phi", pair, False)
+            for block in SCALE_BEHIND_STAGE1.get(step, ()):
+                scale_cr(block)
+            if step == QUARTERS - 1:
+                for j in range(COLUMN_TILES):
+                    root_half(0, j)
 
-        n_grouped = keep.tile([P, PASSES, C, 4], BF16, name="n_grouped", align_bytes=64)
+        for i in range(3):
+            turn_next()
+        hold_clock(1)
+        for j in range(COLUMN_TILES):
+            root_half(1, j)
+            nc.gpsimd.tensor_tensor(out=totals[j][:], in0=sums[:, j, 0:1], in1=sums[:, j, 1:2], op=ALU.add)
+            nc.gpsimd.tensor_scalar(out=means[j][:], in0=totals[j][:], scalar1=1.0 / F, scalar2=0.0, op0=ALU.mult, op1=ALU.add)
+            nc.vector.scalar_tensor_tensor(
+                out=n1[j][:], in0=u1[:, j, :], scalar=means[j][:], in1=gain[:], op0=ALU.subtract, op1=ALU.mult
+            )
+        turn_next()
+        hold_clock(1)
+        n_grouped = keep.tile([P, PASSES, C, PACK], BF16, name="n_grouped", align_bytes=64)
+        for j in range(COLUMN_TILES):
+            bank = transpose_rows(n1[j][:].bitcast(F32))
+            copy_out("S", interleaved(n_grouped, P * j, P), bank[:].rearrange("p (g u) n -> p g n u", u=2))
+            hold_clock(1)
+        pack("cim", 1)
+        pack("cr", 0)
+        n_packed = [quantise(n_grouped[:, g].rearrange("p n t -> p (n t)"), "n", 2) for g in range(PASSES)]
+        turn_next()
+        hold_clock(1)
+        pack("cr", 1)
+        pack("cim", 2)
+        scale_cr(7)
 
-        def turn_n(j, engine):
-            engine = pick(engine)
-            bank = psum.tile([P, 4, P], F32, name="turned", tag="turned", bufs=4)
+        def product(kind, block):
+            bank = product_bank()
             for g in range(PASSES):
-                for u in range(2):
-                    nc.tensor.transpose(bank[:, 2 * g + u, :], n1[j][:, g, u, :].bitcast(F32), ident[:])
-            dst = n_grouped[:].rearrange("p g n t -> p (g n t)").bitcast(F32).rearrange("p (g n u) -> p g n u", g=PASSES, u=2)[:, :, j * P : (j + 1) * P, :]
-            src = bank[:].rearrange("p (g u) n -> p g n u", u=2)
-            if engine == "S":
-                nc.scalar.copy(out=dst, in_=src)
-            else:
-                nc.vector.tensor_copy(out=dst, in_=src)
-
-        turn(("cim", 2), "SS")
-        keep_clock(CFG["clkc"])
-        hook("c0")
-        for j in range(4):
-            half_sqrt(1, j)
-            centre(j)
-        turn(("cr", 1), "SS")
-        keep_clock(CFG["clkc"])
-        for j in range(4):
-            turn_n(j, "S")
-            keep_clock(CFG["clkn"])
-        hook("c1")
-        pack(("cr", 0))
-        nq = [quantise(n_grouped[:, g].rearrange("p n t -> p (n t)"), "n", 2) for g in range(PASSES)]
-        turn(("cim", 3), "SS")
-        keep_clock(CFG["clkc"])
-        pack(("cr", 1))
-        pack(("cim", 2))
-        hook("c2")
-
-        def product(weights, m):
-            bank = psum.tile([P, 512], F32, name="unit", tag="unit", bufs=4)
-            lo = (m % 2) * P
-            for g in range(PASSES):
-                mx(bank[:], weights[m // 2], slice(g * 256 + lo, g * 256 + lo + P), nq[g], slice(0, C), g == 0, g == 1)
+                first = PAIR * g + P * (block % 2)
+                mx(bank[:], packed[kind, block // 2], slice(first, first + P), n_packed[g], slice(0, C), g)
             return bank
 
-        def first_order(t):
-            bank = product(ready["phi"], t)
-            res = stage.tile([P, C], F32, name="s1_out", tag="s1_out", bufs=2, align_bytes=64)
-            (nc.scalar.copy if pick("V") == "S" else nc.vector.tensor_copy)(out=res[:], in_=bank[:])
-            nc.sync.dma_start(out=out_0[t * P : (t + 1) * P, :], in_=res[:])
+        def first_order(block):
+            bank = product("phi", block)
+            result = stage.tile([P, C], F32, name="s1_rows", tag="s1_rows", bufs=2, align_bytes=64)
+            nc.vector.tensor_copy(out=result[:], in_=bank[:])
+            nc.sync.dma_start(out=out_0[block * P : (block + 1) * P, :], in_=result[:])
 
-        def finish(m, sq):
-            res = stage.tile([P, C], F32, name="u2_out", tag="u2_out", bufs=3, align_bytes=64)
-            nc.scalar.activation(out=res[:], in_=sq[:, 0, :], func=ACT.Sqrt, bias=quarter[:])
-            nc.sync.dma_start(out=out_1[m * P : (m + 1) * P, :], in_=res[:])
+        def finish(block, squares):
+            result = stage.tile([P, C], F32, name="u2_rows", tag="u2_rows", bufs=3, align_bytes=64)
+            nc.scalar.activation(out=result[:], in_=squares[:, 0, :], func=ACT.Sqrt, bias=quarter[:])
+            nc.sync.dma_start(out=out_1[block * P : (block + 1) * P, :], in_=result[:])
 
-        carried = [("phi", 0), ("cr", 2), ("phi", 1), ("cr", 3)]
-        if CFG["car"]:
-            carried = [("cr", 2), ("phi", 0), ("cr", 3), ("phi", 1)]
-        waiting = ("cim", 3)
-        prev = None
-        for m in range(8):
-            banks = [product(ready["cr"], m), product(ready["cim"], m)]
-            if m == 7 and CFG["split"]:
-                finish(prev[0], prev[1])
-                sq = stage.tile([P, 2, C], F32, name="sq2", tag="sq2", bufs=3, align_bytes=64)
-                res = stage.tile([P, C], F32, name="u2_out", tag="u2_out", bufs=3, align_bytes=64)
-                for z in range(2):
-                    cols = slice(256 * z, 256 * z + 256)
-                    for i in range(2):
-                        nc.scalar.activation(out=sq[:, i, cols], in_=banks[i][:, cols], func=ACT.Square)
-                    nc.vector.tensor_tensor(out=sq[:, 0, cols], in0=sq[:, 0, cols], in1=sq[:, 1, cols], op=ALU.add)
-                for z in range(2):
-                    cols = slice(256 * z, 256 * z + 256)
-                    nc.scalar.activation(out=res[:, cols], in_=sq[:, 0, cols], func=ACT.Sqrt, bias=quarter[:])
-                    nc.sync.dma_start(out=out_1[m * P : (m + 1) * P, cols], in_=res[:, cols])
-                break
-            sq = stage.tile([P, 2, C], F32, name="sq2", tag="sq2", bufs=3, align_bytes=64)
+        last_turned = ("cim", 3)
+        unfinished = None
+        for block in range(G // P):
+            banks = [product("cr", block), product("cim", block)]
+            squares = stage.tile([P, 2, C], F32, name="squares", tag="squares2", bufs=4, align_bytes=64)
             for i in range(2):
-                nc.scalar.activation(out=sq[:, i, :], in_=banks[i][:], func=ACT.Square)
-            hook("m%d" % m)
-            if waiting is not None:
-                pack(waiting)
-                waiting = None
-            nc.vector.tensor_tensor(out=sq[:, 0, :], in0=sq[:, 0, :], in1=sq[:, 1, :], op=ALU.add)
-            if m < len(carried):
-                turn(carried[m], "SS")
-                waiting = carried[m]
-            if prev is not None:
-                finish(prev[0], prev[1])
-            prev = (m, sq)
-            for t in range(4):
-                if CFG["fo"][t] == m or (m == 6 and CFG["fo"][t] == 7):
-                    first_order(t)
-        if not CFG["split"]:
-            finish(prev[0], prev[1])
+                nc.scalar.activation(out=squares[:, i, :], in_=banks[i][:], func=ACT.Square)
+            for cr_block in SCALE_WITHIN_STAGE2.get(block, ()):
+                scale_cr(cr_block)
+            if last_turned is not None:
+                pack(last_turned[0], last_turned[1])
+                last_turned = None
+            nc.vector.tensor_tensor(out=squares[:, 0, :], in0=squares[:, 0, :], in1=squares[:, 1, :], op=ALU.add)
+            if pairs_to_turn:
+                last_turned = pairs_to_turn[0]
+                turn_next()
+            if unfinished is not None:
+                finish(unfinished[0], unfinished[1])
+            unfinished = (block, squares)
+            for s1_block in FIRST_ORDER_BEHIND.get(block, ()):
+                first_order(s1_block)
+        finish(unfinished[0], unfinished[1])

from contextlib import ExitStack

import concourse.mybir as mybir
from concourse.masks import make_identity

S, F, G, T, C = 1024, 1024, 1024, 512, 512
FLOPS = 2 * C * (2 * F * S + 2 * G * F + T * F)

F32 = mybir.dt.float32
BF16 = mybir.dt.bfloat16
U32 = mybir.dt.uint32
U8 = mybir.dt.uint8
FP8 = mybir.dt.float8_e4m3fn
FP8X4 = mybir.dt.float8_e4m3fn_x4
ACT = mybir.ActivationFunctionType
ALU = mybir.AluOpType

P = 128
PACK = 4
PASSES = 2
K_PASS = P * PACK
PAIR = 2 * P
BANK = 512
COLUMN_TILES = C // P
QUARTERS = F // PAIR

WEIGHT_PAIRS = (
    ("ar", 0, "SS"),
    ("aim", 0, "SS"),
    ("ar", 1, "SS"),
    ("aim", 1, "SS"),
    ("ar", 2, "SS"),
    ("aim", 2, "VS"),
    ("ar", 3, "VV"),
    ("aim", 3, "SS"),
    ("cim", 0, "SS"),
    ("cim", 1, "SS"),
    ("cr", 0, "VS"),
    ("cim", 2, "VV"),
    ("cr", 1, "SS"),
    ("cim", 3, "SS"),
    ("phi", 0, "SV"),
    ("cr", 2, "SS"),
    ("phi", 1, "VV"),
    ("cr", 3, "SS"),
)
HEAD_PAIRS = 3
STAGE1_PAIRS = 6
SCALE_BEHIND_STAGE1 = {1: (2,), 3: (1, 5), 5: (3, 4)}
SCALE_WITHIN_STAGE2 = {1: (6,)}
FIRST_ORDER_BEHIND = {3: (0,), 4: (1,), 6: (2, 3)}


def tile_learnedsecondorderscattering_kernel(tc, x, ar, aim, g1, cr_bytes, cr_scale, cim, phi, out_0, out_1):
    nc = tc.nc
    with ExitStack() as ctx:
        keep = ctx.enter_context(tc.tile_pool(name="keep", bufs=1))
        stage = ctx.enter_context(tc.tile_pool(name="stage", bufs=1))
        psum = ctx.enter_context(tc.psum_pool(name="psum", bufs=1))
        ctx.enter_context(tc.manual_schedule())

        scale_cols = keep.tile([P, 8], F32, name="scale_cols")
        gain_cols = keep.tile([P, 8], BF16, name="gain_cols")
        nc.scalar.dma_start(out=scale_cols[:], in_=cr_scale.rearrange("o (n c) -> n (o c)", c=8))
        nc.scalar.dma_start(out=gain_cols[:], in_=g1.rearrange("(n c) -> n c", c=8))

        x_rows = {}
        weight_rows = {}
        cr_codes = {}

        def load_x(g):
            x_rows[g] = keep.tile([P, PACK, C], BF16, name="x_rows%d" % g, align_bytes=64)
            nc.sync.dma_start(out=x_rows[g][:], in_=x.rearrange("(g p t) n -> g p t n", p=P, t=PACK)[g])

        def load_pair(kind, pair, by_block):
            matrix = {"ar": ar, "aim": aim, "cim": cim, "phi": phi}[kind]
            rows = stage.tile([P, 2, S], BF16, name="rows", tag="rows", bufs=10, align_bytes=64)
            source = matrix[pair * PAIR : (pair + 1) * PAIR, :].rearrange("(b p) k -> p b k", b=2)
            if by_block:
                for b in range(2):
                    nc.sync.dma_start(out=rows[:, b, :], in_=source[:, b, :])
            else:
                nc.sync.dma_start(out=rows[:], in_=source)
            weight_rows[kind, pair] = rows

        def load_cr(half):
            cr_codes[half] = keep.tile([P, 4, F], U8, name="cr_codes%d" % half, align_bytes=64)
            source = cr_bytes[half * 4 * P : (half + 1) * 4 * P, :].rearrange("(b p) k -> p b k", b=4)
            nc.sync.dma_start(out=cr_codes[half][:], in_=source)

        load_x(0)
        load_pair("ar", 0, True)
        load_x(1)
        load_pair("aim", 0, True)
        for q in range(1, QUARTERS):
            load_pair("ar", q, q < 2)
            load_pair("aim", q, q < 2)
            if q < 3:
                load_cr(q - 1)

        identity = keep.tile([P, P], F32, name="identity", align_bytes=64)
        make_identity(nc, identity[:])
        quarter = keep.tile([P, 1], F32, name="quarter")
        nc.vector.memset(quarter[:], 0.25)
        filler = keep.tile([P, C], BF16, name="filler", align_bytes=64)
        nc.vector.memset(filler[:], 0.0)
        first_root = keep.tile([P, 1], F32, name="first_root")
        nc.scalar.activation(out=first_root[:], in_=quarter[:], func=ACT.Sqrt)
        scale_spread = stage.tile([P, 8, P], F32, name="scale_spread", tag="squares2", bufs=4, align_bytes=64)
        gain_spread = stage.tile([P, 8, P], F32, name="gain_spread", tag="squares2", bufs=4, align_bytes=64)
        nc.vector.tensor_copy(out=scale_spread[:], in_=scale_cols[:].unsqueeze(2).to_broadcast([P, 8, P]))
        nc.vector.tensor_copy(out=gain_spread[:], in_=gain_cols[:].unsqueeze(2).to_broadcast([P, 8, P]))
        gain = keep.tile([P, F], F32, name="gain", align_bytes=64)
        scale = keep.tile([P, F], F32, name="scale", align_bytes=64)

        def product_bank():
            return psum.tile([P, BANK], F32, name="product", tag="product", bufs=4)

        def transpose_bank():
            return psum.tile([P, 4, P], F32, name="turned", tag="turned", bufs=4)

        def hold_clock(n):
            for i in range(n):
                bank = product_bank()
                nc.tensor.matmul(bank[:], lhsT=filler[:, 0:P], rhs=filler[:], start=True, stop=True)

        def copy_out(engine, out, in_):
            if engine == "S":
                nc.scalar.copy(out=out, in_=in_)
            else:
                nc.vector.tensor_copy(out=out, in_=in_)

        def transpose_rows(words):
            bank = transpose_bank()
            for g in range(PASSES):
                for u in range(2):
                    nc.tensor.transpose(bank[:, 2 * g + u, :], words[:, 256 * g + u : 256 * (g + 1) : 2], identity[:])
            return bank

        def interleaved(grouped, first, width):
            words = grouped[:].rearrange("p g r t -> p (g r t)").bitcast(F32)
            words = words.rearrange("p (g r u) -> p g r u", g=PASSES, u=2)
            return words[:, :, first : first + width, :]

        def quantise(flat, tag, bufs):
            width = flat.shape[1] // PACK
            codes = keep.tile([P, width], U32, name="codes", tag=tag + "_codes", bufs=bufs, align_bytes=64)
            scales = keep.tile([P, width], U8, name="scales", tag=tag + "_scales", bufs=bufs, align_bytes=64)
            nc.vector.quantize_mx(out=codes[:].bitcast(FP8X4), scales=scales[:], in_=flat)
            return codes, scales

        def mx(out, left, left_cols, right, right_cols, g):
            nc.tensor.matmul_mx(
                out=out,
                lhsT=left[0][:, left_cols].bitcast(FP8X4),
                lhsT_scale=left[1][:, left_cols],
                rhs=right[0][:, right_cols].bitcast(FP8X4),
                rhs_scale=right[1][:, right_cols],
                start=g == 0,
                stop=g == PASSES - 1,
            )

        cr_scaled = {}

        def scale_cr(block):
            rows = stage.tile([P, F], BF16, name="cr_scaled", tag="cr_scaled", bufs=8, align_bytes=64)
            codes = cr_codes[block // 4][:, block % 4, :]
            nc.vector.tensor_tensor(out=rows[:], in0=codes.bitcast(FP8), in1=scale[:], op=ALU.mult)
            cr_scaled[block] = rows

        pairs_to_turn = list(WEIGHT_PAIRS)
        turned = {}
        packed = {}
        packed_bufs = {"ar": 4, "aim": 4, "cim": 4, "cr": 4, "phi": 2}

        def turn_next():
            kind, pair, engines = pairs_to_turn[0]
            pairs_to_turn.remove(pairs_to_turn[0])
            grouped = stage.tile([P, PASSES, PAIR, PACK], BF16, name="grouped", tag="grouped", bufs=6, align_bytes=64)
            for b in range(2):
                block = cr_scaled[2 * pair + b][:] if kind == "cr" else weight_rows[kind, pair][:, b, :]
                bank = transpose_rows(block.bitcast(F32))
                copy_out(engines[b], interleaved(grouped, b * P, P), bank[:].rearrange("p (g u) r -> p g r u", u=2))
            turned[kind, pair] = grouped

        def pack(kind, pair):
            packed[kind, pair] = quantise(turned[kind, pair][:].rearrange("p g r t -> p (g r t)"), kind, packed_bufs[kind])

        hold_clock(1)
        for spread, vector in ((scale_spread, scale), (gain_spread, gain)):
            for half in range(2):
                bank = transpose_bank()
                for i in range(4):
                    nc.tensor.transpose(bank[:, i, :], spread[:, 4 * half + i, :], identity[:])
                columns = vector[:].rearrange("p (n c) -> p n c", c=8)[:, :, 4 * half : 4 * half + 4]
                nc.scalar.copy(out=columns, in_=bank[:].rearrange("p c n -> p n c"))

        x_grouped = []
        for g in range(PASSES):
            grouped = stage.tile([P, C, PACK], BF16, name="x_grouped", tag="x_grouped", bufs=2, align_bytes=64)
            nc.vector.tensor_copy(
                out=grouped[:].rearrange("p (c i) t -> p c t i", i=4),
                in_=x_rows[g][:].rearrange("p t (c i) -> p c t i", i=4),
            )
            x_grouped.append(grouped)
        x_packed = [quantise(grouped[:].rearrange("p n t -> p (n t)"), "x", 2) for grouped in x_grouped]

        turn_next()
        turn_next()
        hold_clock(2)
        pack("ar", 0)
        pack("aim", 0)
        scale_cr(0)
        turn_next()
        for pair in range(4):
            load_pair("cim", pair, False)

        u1 = keep.tile([P, COLUMN_TILES, F], F32, name="u1", align_bytes=64)
        n1 = [keep.tile([P, F], BF16, name="n1_%d" % j, align_bytes=64) for j in range(COLUMN_TILES)]
        sums = keep.tile([P, COLUMN_TILES, 2], F32, name="sums")
        totals = [keep.tile([P, 1], F32, name="total_%d" % j) for j in range(COLUMN_TILES)]
        means = [keep.tile([P, 1], F32, name="mean_%d" % j) for j in range(COLUMN_TILES)]

        def root_half(half, j):
            view = u1[:, j, F // 2 * half : F // 2 * (half + 1)]
            nc.scalar.activation(out=view, in_=view, func=ACT.Sqrt, bias=quarter[:], accum_out=sums[:, j, half : half + 1])

        for step in range(2 * QUARTERS):
            q, side = step // 2, step % 2
            banks = []
            for j in (2 * side, 2 * side + 1):
                bank = product_bank()
                for part, kind in enumerate(("ar", "aim")):
                    for g in range(PASSES):
                        f_cols = slice(PAIR * g, PAIR * (g + 1))
                        mx(bank[:, PAIR * part : PAIR * (part + 1)], x_packed[g], slice(P * j, P * (j + 1)), packed[kind, q], f_cols, g)
                banks.append(bank)
            squares = stage.tile([P, 2, BANK], F32, name="squares", tag="squares2", bufs=4, align_bytes=64)
            for i in range(2):
                nc.scalar.activation(out=squares[:, i, :], in_=banks[i][:], func=ACT.Square)
            if step < STAGE1_PAIRS + 1:
                pack(WEIGHT_PAIRS[step + 2][0], WEIGHT_PAIRS[step + 2][1])
            nc.vector.tensor_tensor(
                out=u1[:, 2 * side : 2 * side + 2, PAIR * q : PAIR * (q + 1)],
                in0=squares[:, :, 0:PAIR],
                in1=squares[:, :, PAIR : 2 * PAIR],
                op=ALU.add,
            )
            if step < STAGE1_PAIRS:
                turn_next()
            if step == 0:
                for pair in range(2):
                    load_pair("phi", pair, False)
            for block in SCALE_BEHIND_STAGE1.get(step, ()):
                scale_cr(block)
            if step == QUARTERS - 1:
                for j in range(COLUMN_TILES):
                    root_half(0, j)

        for i in range(3):
            turn_next()
        hold_clock(1)
        for j in range(COLUMN_TILES):
            root_half(1, j)
            nc.gpsimd.tensor_tensor(out=totals[j][:], in0=sums[:, j, 0:1], in1=sums[:, j, 1:2], op=ALU.add)
            nc.gpsimd.tensor_scalar(out=means[j][:], in0=totals[j][:], scalar1=1.0 / F, scalar2=0.0, op0=ALU.mult, op1=ALU.add)
            nc.vector.scalar_tensor_tensor(
                out=n1[j][:], in0=u1[:, j, :], scalar=means[j][:], in1=gain[:], op0=ALU.subtract, op1=ALU.mult
            )
        turn_next()
        hold_clock(1)
        n_grouped = keep.tile([P, PASSES, C, PACK], BF16, name="n_grouped", align_bytes=64)
        for j in range(COLUMN_TILES):
            bank = transpose_rows(n1[j][:].bitcast(F32))
            copy_out("S", interleaved(n_grouped, P * j, P), bank[:].rearrange("p (g u) n -> p g n u", u=2))
            hold_clock(1)
        pack("cim", 1)
        pack("cr", 0)
        n_packed = [quantise(n_grouped[:, g].rearrange("p n t -> p (n t)"), "n", 2) for g in range(PASSES)]
        turn_next()
        hold_clock(1)
        pack("cr", 1)
        pack("cim", 2)
        scale_cr(7)

        def product(kind, block):
            bank = product_bank()
            for g in range(PASSES):
                first = PAIR * g + P * (block % 2)
                mx(bank[:], packed[kind, block // 2], slice(first, first + P), n_packed[g], slice(0, C), g)
            return bank

        def first_order(block):
            bank = product("phi", block)
            result = stage.tile([P, C], F32, name="s1_rows", tag="s1_rows", bufs=2, align_bytes=64)
            nc.vector.tensor_copy(out=result[:], in_=bank[:])
            nc.sync.dma_start(out=out_0[block * P : (block + 1) * P, :], in_=result[:])

        def finish(block, squares):
            result = stage.tile([P, C], F32, name="u2_rows", tag="u2_rows", bufs=3, align_bytes=64)
            nc.scalar.activation(out=result[:], in_=squares[:, 0, :], func=ACT.Sqrt, bias=quarter[:])
            nc.sync.dma_start(out=out_1[block * P : (block + 1) * P, :], in_=result[:])

        last_turned = ("cim", 3)
        unfinished = None
        for block in range(G // P):
            banks = [product("cr", block), product("cim", block)]
            squares = stage.tile([P, 2, C], F32, name="squares", tag="squares2", bufs=4, align_bytes=64)
            for i in range(2):
                nc.scalar.activation(out=squares[:, i, :], in_=banks[i][:], func=ACT.Square)
            for cr_block in SCALE_WITHIN_STAGE2.get(block, ()):
                scale_cr(cr_block)
            if last_turned is not None:
                pack(last_turned[0], last_turned[1])
                last_turned = None
            nc.vector.tensor_tensor(out=squares[:, 0, :], in0=squares[:, 0, :], in1=squares[:, 1, :], op=ALU.add)
            if pairs_to_turn:
                last_turned = pairs_to_turn[0]
                turn_next()
            if unfinished is not None:
                finish(unfinished[0], unfinished[1])
            unfinished = (block, squares)
            for s1_block in FIRST_ORDER_BEHIND.get(block, ()):
                first_order(s1_block)
        finish(unfinished[0], unfinished[1])
